import numpy as np, ml_dtypes
CORES = [9,17,57,81,121,137,145,185,209,249]
N = 10
import mx_ref
NC, G, D = 128, 2, 64
C = np.float32(0.031)
BF = ml_dtypes.bfloat16
def cut(t, i, w=512):
    return t[:, w * i:w * i + w]
def tile(rs):
    return np.stack(rs, axis=2).reshape(128, -1).astype(BF)
def layer(w, X):
    out = []
    for i in range(G):
        for t in range(len(X)):
            p = mx_ref.matmul(mx_ref.quantize(cut(w, len(X) * i + t)), X[t])
            z = p if t == 0 else z + p
        out.append(z)
    return out
def act(Z):
    return [np.maximum(s * z, 0) * C for z in Z for s in (1, -1)]
def setup_inputs(rng):
    def f(*shape):
        return mx_ref.flush((rng.standard_normal(shape, dtype=np.float32) * np.exp2(rng.integers(-2, 3, shape[:-1] + (1,)))).astype(BF))
    return {"x": f(N, 128, 4 * NC), "w1": f(N, 128, G * 512), "wt": f(N, 128, 3 * 512)}
def setup_inputs_blocks(rng):
    d = setup_inputs(rng)
    for k in ("x", "wt", "w1"): d[k] = mx_ref.spread(d[k], rng, 2)
    return d
def setup_inputs_wide(rng):
    d = setup_inputs(rng)
    for k in ("wt",): d[k] = mx_ref.flush((d[k].astype(np.float32) * np.exp2(rng.integers(-6, 7, (N, 1, 1))).astype(np.float32)).astype(BF))
    return d
def setup_inputs_zeros(rng):
    d = setup_inputs(rng); v = d["x"].reshape(N, 128, -1, 4).copy()
    v[np.broadcast_to((rng.random((N, 1, v.shape[2], 1)) < 0.33), v.shape)] = 0
    d["x"] = v.reshape(d["x"].shape)
    return d
def reference(x, w1, wt):
    h = [tile(act(layer(w1[j], [mx_ref.quantize(x[j])]))) for j in range(N)]
    y = np.zeros((N, 128, NC), np.float32)
    for r in range(N):
        e = np.concatenate([h[(r - 1) % N][:, 4 * (NC - D):], h[r], h[(r + 1) % N][:, :4 * D]], axis=1)
        for t in range(3):
            p = mx_ref.matmul(mx_ref.quantize(cut(wt[r], t)), mx_ref.quantize(e[:, 4 * D * t:4 * D * t + 4 * NC]))
            y[r] = p if t == 0 else y[r] + p
    return {"y": y}

import numpy as np
from concourse.bass import DstId, RemoteDMATransfer
from concourse.mybir import dt, AluOpType, ActivationFunctionType

X4, U8, BF, F32 = "float8_e4m3fn_x4", "uint8", "bfloat16", "float32"
NC, D = 128, 64
C = float(np.float32(0.031))
SIM = 256

SCRATCH = {
    "xt": ("sbuf", [128, 512], BF),
    "w1t": ("sbuf", [128, 1024], BF),
    "wtt": ("sbuf", [128, 1536], BF),
    "ht": ("sbuf", [128, 512], BF),
    "yo": ("sbuf", [128, NC], F32),
    "xq": ("sbuf", [128, NC], X4),
    "w1q": ("sbuf", [128, 256], X4),
    "w1p": ("sbuf", [128, 128], U8),
    "wq": ("sbuf", [128, 384], X4),
    "wp": ("sbuf", [128, 384], U8),
    "hs": ("sbuf", [128, NC], X4),
    "sp": ("sbuf", [128, 3 * NC], U8),
    "e": ("sbuf", [128, NC + 2 * D], X4),
    "ep": ("sbuf", [128, NC + 2 * D], U8),
    "rc": ("sbuf", [128, D], X4),
    "rp": ("sbuf", [128, 4 * D], U8),
    "z0": ("psum", [128, 512], F32),
    "z1": ("psum", [128, 512], F32),
    "yp": ("psum", [128, 512], F32),
}
SEMAPHORES = ["lx", "lw0", "lw1", "lwt", "qx", "qw0", "qw1", "qwt", "z0", "z1", "act", "hq", "he", "y", "yo", "yst",
              "below", "above", "relay", "sent"]


def bits(m):
    return [1 << k for k in range(16) if m >> k & 1]


def helpers(topo, src, dst, near):
    return [c for c in range(SIM) if c != src and topo.host(c) == topo.host(src) and topo.chip(c) == topo.chip(src)
            and (topo.die(c) == topo.die(src)) == near and topo.may_write(c, dst)][:2]


def codes(t, a, b):
    return t[:, a:b].bitcast(dt.uint8)


SRC = {1: (NC - D, NC), 0: (0, D)}
WIN = {1: (0, 2 * NC), 0: (NC, 3 * NC)}
PICK = {1: (2 * NC - D, 2 * NC), 0: (0, D)}
DST = {1: (0, D), 0: (D + NC, NC + 2 * D)}
ARR = {1: "below", 0: "above"}


def helper_program(g, core, T, topo, dst, d, kind):
    rid, pid = topo.addr(dst, core)
    m = topo.mask(core, dst)
    g.wait_ge(T.sem.relay, RELAY_ENGINES)
    if kind == 0:
        out, src = codes(T.e, *DST[d]), codes(T.rc, 0, D)
    else:
        out, src = T.ep[:, DST[d][0]:DST[d][1]], T.rp[:, PICK[d][0]:PICK[d][1]]
    g.remote_dma(out, src, T.sem[ARR[d]], T.sem.sent, pid, rid, m)
    g.wait_ge(T.sem.sent, len(bits(m)))


RELAY_ENGINES = 4


def rank_program(g, core, T, topo):
    n = len(T.cores)
    rank = T.rank_of(core)
    if rank is None:
        for r, src in enumerate(T.cores):
            if (topo.host(src), topo.chip(src)) != (topo.host(core), topo.chip(core)):
                continue
            for d in (1, 0):
                dst = T.cores[(r + (1 if d else -1)) % n]
                if not topo.may_write(src, dst):
                    hs = helpers(topo, src, dst, d == 1)
                    if core in hs:
                        helper_program(g, core, T, topo, dst, d, hs.index(core))
        return

    to = {1: T.cores[(rank + 1) % n], 0: T.cores[(rank - 1) % n]}
    direct = [d for d in (1, 0) if topo.may_write(core, to[d])]
    by_helper = [d for d in (0, 1) if d not in direct]
    S = T.sem

    g.sync.dma_start(T.xt[:], T.x[:]).then_inc(S.lx, 16)
    g.scalar.dma_start(T.w1t[:, 0:512], T.w1[:, 0:512]).then_inc(S.lw0, 16)
    g.sync.dma_start(T.w1t[:, 512:1024], T.w1[:, 512:1024]).then_inc(S.lw1, 16)
    g.sync.dma_start(T.wtt[:], T.wt[:]).then_inc(S.lwt, 16)

    v = g.vector
    v.wait_ge(S.lx, 16)
    v.quantize_mx(T.xq[:], T.sp[:, 0:NC], T.xt[:]).then_inc(S.qx, 1)
    v.wait_ge(S.lw0, 16)
    v.quantize_mx(T.w1q[:, 0:128], T.sp[:, 2 * NC:3 * NC], T.w1t[:, 0:512]).then_inc(S.qw0, 1)
    v.wait_ge(S.lw1, 16)
    v.quantize_mx(T.w1q[:, 128:256], T.w1p[:], T.w1t[:, 512:1024]).then_inc(S.qw1, 1)
    v.wait_ge(S.z1, 1)
    for b, c in ((2, C), (3, -C)):
        v.tensor_scalar(T.ht[:, b:512:4], T.z1[:, 0:NC], c, 0.0, AluOpType.mult, AluOpType.max).then_inc(S.act, 1)
    v.wait_ge(S.act, 4)
    v.quantize_mx(T.hs[:], T.sp[:, NC:2 * NC], T.ht[:]).then_inc(S.hq, 1)
    v.quantize_mx(T.e[:, D:D + NC], T.ep[:, D:D + NC], T.ht[:]).then_inc(S.he, 1)
    v.wait_ge(S.lwt, 16)
    v.quantize_mx(T.wq[:], T.wp[:], T.wtt[:]).then_inc(S.qwt, 1)
    v.wait_ge(S.y, 1)
    v.tensor_copy(T.yo[:], T.yp[:, 0:NC]).then_inc(S.yo, 1)

    a = g.scalar
    a.wait_ge(S.z0, 1)
    for b, c in ((0, C), (1, -C)):
        a.activation(T.ht[:, b:512:4], T.z0[:, 0:NC], ActivationFunctionType.Relu, scale=c).then_inc(S.act, 1)

    t = g.tensor
    t.wait_ge(S.qx, 1)
    t.wait_ge(S.qw0, 1)
    t.matmul_mx(T.z0[:, 0:NC], T.w1q[:, 0:128], T.sp[:, 2 * NC:3 * NC], T.xq[:], T.sp[:, 0:NC], True, True).then_inc(S.z0, 1)
    t.wait_ge(S.qw1, 1)
    t.matmul_mx(T.z1[:, 0:NC], T.w1q[:, 128:256], T.w1p[:], T.xq[:], T.sp[:, 0:NC], True, True).then_inc(S.z1, 1)

    def tap(k, first, last):
        return t.matmul_mx(T.yp[:, 0:NC], T.wq[:, 128 * k:128 * k + 128], T.wp[:, 128 * k:128 * k + 128],
                           T.e[:, D * k:D * k + NC], T.ep[:, D * k:D * k + NC], first, last)
    t.wait_ge(S.he, 1)
    t.wait_ge(S.qwt, 1)
    tap(1, True, False)
    order = [(0, 1), (2, 0)]
    if topo.may_write(to[1], core):
        order = order[::-1]
    for i, (k, d) in enumerate(order):
        src = to[1 - d]
        if topo.may_write(src, core):
            cnt = 2 * len(bits(topo.mask(src, core)))
        else:
            cnt = sum(len(bits(topo.mask(c, core))) for c in helpers(topo, src, core, d == 1))
        t.wait_ge(S[ARR[d]], cnt)
        last = tap(k, False, i == 1)
    last.then_inc(S.y, 1)

    g.wait_ge(S.hq, 1)
    sent = 0
    free = {}
    for d in by_helper:
        hs = helpers(topo, core, to[d], d == 1)
        m = topo.mask(core, hs[0])
        for e in direct:
            m &= ~topo.mask(core, to[e])
        mine = bits(m)[by_helper.index(d)::len(by_helper)]
        free[d] = (hs, mine[:RELAY_ENGINES], mine[RELAY_ENGINES:2 * RELAY_ENGINES])
    out = []
    for d in by_helper:
        hs, ec, es = free[d]
        for c, m, src, dst in ((hs[0], ec, codes(T.hs, *SRC[d]), codes(T.rc, 0, D)),
                               (hs[1], es, T.sp[:, WIN[d][0]:WIN[d][1]], T.rp[:])):
            rid, pid = topo.addr(c, core)
            out.append(RemoteDMATransfer(dst_ids=[DstId(rid=rid, pnc=pid)], dma_engine_mask=sum(m), remote_sem=S.relay,
                                         src=src, dst=dst))
            sent += len(m)
    g.remote_dma_fused(out, local_sem=S.sent)
    for d in direct:
        rid, pid = topo.addr(to[d], core)
        m = topo.mask(core, to[d])
        s0, s1 = SRC[d]
        g.remote_dma(codes(T.e, *DST[d]), codes(T.hs, s0, s1), S[ARR[d]], S.sent, pid, rid, m)
        g.remote_dma(T.ep[:, DST[d][0]:DST[d][1]], T.sp[:, NC + s0:NC + s1], S[ARR[d]], S.sent, pid, rid, m)
        sent += 2 * len(bits(m))
    g.wait_ge(S.sent, sent)

    g.sync.wait_ge(S.yo, 1)
    g.sync.dma_start(T.y[:], T.yo[:]).then_inc(S.yst, 16)
    g.sync.wait_ge(S.yst, 16)
